import numpy as np
import ml_dtypes


def mxq(x, axis, fmt="e4m3"):
    dtype, down = {"e4m3": (ml_dtypes.float8_e4m3fn, 7), "e5m2": (ml_dtypes.float8_e5m2, 14)}[fmt]
    v = np.moveaxis(np.asarray(x, np.float32).astype(ml_dtypes.bfloat16).astype(np.float64), axis, -1)
    blocks = v.reshape(v.shape[:-1] + (-1, 32))
    amax = np.abs(blocks).max(-1, keepdims=True)
    byte = np.maximum(np.where(amax > 0, np.frexp(amax)[1] - 1 + 127, 0) - down, 1)
    scale = np.exp2(byte - 127.0)
    codes = (blocks / scale).astype(np.float32).astype(dtype).astype(np.float64)
    return np.moveaxis((codes * scale).reshape(v.shape), -1, axis)


WIDE = False


def mx_kscale(k):
    if not WIDE:
        return np.ones(k)
    levels = np.array([10, -10, 5, -5, 0])
    if k % 512:
        return np.exp2(np.random.permutation(np.resize(levels, k // 32))).repeat(32)
    a = np.empty((k // 512, 16))
    for p in range(k // 512):
        a[p, :8] = np.random.permutation(np.resize(levels, 8))
        for g in range(8):
            far = levels[np.abs(levels - a[p, g]) >= 10]
            a[p, g + 8] = far[np.random.randint(len(far))]
    return np.exp2(a.ravel()).repeat(32)


def f64(x):
    return np.asarray(x).astype(np.float64)


def striped8(idx):
    return np.asarray(idx).reshape(8, -1, 16).transpose(0, 2, 1).reshape(128, -1).astype(np.uint16)


def unstriped8(offs):
    return offs.reshape(8, 16, -1).transpose(0, 2, 1).reshape(8, -1).astype(np.int64)


def pick8(x, idx, run):
    r = np.arange(len(x))
    return x[r[:, None], idx[r % (8 * run) // run]]


E2M1 = np.array([0.0, 0.5, 1.0, 1.5, 2.0, 3.0, 4.0, 6.0, -0.0, -0.5, -1.0, -1.5, -2.0, -3.0, -4.0, -6.0])


def pack_weight(w, fmt):
    k, n = w.shape
    w = f64(np.asarray(w, np.float32).astype(ml_dtypes.bfloat16)).reshape(k // 32, 32, n)
    amax = np.abs(w).max(1)
    if fmt == "e4m3":
        byte = np.frexp(amax)[1] - 1 + 127 - 7
    else:
        mant, ex = np.frexp(amax / 6.0)
        byte = np.where(mant > 0.5, ex, ex - 1) + 127
    byte = np.clip(np.where(amax > 0, byte, 1), 1, 254)
    scaled = (w * np.exp2(127.0 - byte)[:, None, :]).reshape(k, n).astype(np.float32)
    by_word = np.ascontiguousarray(scaled.reshape(k // 512, 128, 4, n).transpose(0, 1, 3, 2))
    if fmt == "e4m3":
        words = by_word.astype(ml_dtypes.float8_e4m3fn).view(np.uint8)
    else:
        c = by_word.astype(ml_dtypes.float4_e2m1fn).view(np.uint8) & 0xF
        words = (c[..., 0::2] | (c[..., 1::2] << 4)).reshape(k // 512, 128, 2 * n)
    return np.ascontiguousarray(words), np.ascontiguousarray(byte.astype(np.uint8).reshape(k // 512, 16, n))


def unpack_weight(words, scales, fmt):
    g, _, n = scales.shape
    words = np.ascontiguousarray(words).reshape(g, 128, n, -1)
    if fmt == "e4m3":
        vals = words.view(ml_dtypes.float8_e4m3fn).astype(np.float64)
    else:
        nib = np.empty((g, 128, n, 4), np.uint8)
        nib[..., 0::2] = words & 0xF
        nib[..., 1::2] = words >> 4
        vals = E2M1[nib]
    vals = vals * np.repeat(np.exp2(scales.astype(np.float64) - 127.0), 8, axis=1)[..., None]
    return vals.transpose(0, 1, 3, 2).reshape(g * 512, n)


D, T, U, X, I, Q = 512, 1024, 1024, 1024, 512, 128


def setup_inputs():
    n = np.random.standard_normal
    idx = np.stack([np.random.permutation(T)[:I] for _ in range(8)])
    idx2 = np.stack([np.random.permutation(U)[:I] for _ in range(8)])
    idx3 = np.stack([np.random.permutation(T)[:I] for _ in range(8)])
    idx4 = np.stack([np.random.permutation(X)[:I] for _ in range(8)])
    idx5 = np.stack([np.random.permutation(X)[:I] for _ in range(8)])
    fd = mx_kscale(D)
    keysp = pack_weight(n((D, T)) / fd[:, None], "e2m1")
    notesp = pack_weight(n((D, U)) / fd[:, None], "e4m3")
    usersp = pack_weight(n((D, X)) / fd[:, None], "e2m1")
    return {
        "query": (n((D, Q)) * 1.0 / np.sqrt(D) * fd[:, None]).astype(np.float32),
        "keys_words": keysp[0],
        "keys_scales": keysp[1],
        "notes_words": notesp[0],
        "notes_scales": notesp[1],
        "users_words": usersp[0],
        "users_scales": usersp[1],
        "offs": striped8(idx),
        "offs2": striped8(idx2),
        "offs3": striped8(idx3),
        "offs4": striped8(idx4),
        "offs5": striped8(idx5),
    }


def reference(query, keys_words, keys_scales, notes_words, notes_scales, users_words, users_scales, offs, offs2, offs3, offs4, offs5):
    idx = unstriped8(offs)
    idx2 = unstriped8(offs2)
    idx3 = unstriped8(offs3)
    idx4 = unstriped8(offs4)
    idx5 = unstriped8(offs5)
    keysu = unpack_weight(keys_words, keys_scales, "e2m1")
    notesu = unpack_weight(notes_words, notes_scales, "e4m3")
    usersu = unpack_weight(users_words, users_scales, "e2m1")
    queryq = mxq(f64(query), 0, "e4m3")
    a = queryq.T @ keysu
    b = queryq.T @ notesu
    c0 = queryq.T @ usersu
    r = pick8(b, idx2, 16) - pick8(a, idx, 16)
    f1 = np.zeros((Q, T))
    f1[np.arange(Q)[:, None], idx[np.arange(Q) % 128 // 16]] = r
    a2 = a + f1
    f2 = np.zeros((Q, X))
    f2[np.arange(Q)[:, None], idx4[np.arange(Q) % 128 // 16]] = pick8(a2, idx3, 16)
    cc = c0 - f2
    y = pick8(cc, idx5, 16)
    return y

@@ -1,0 +1,147 @@
+from contextlib import ExitStack
+
+import concourse.mybir as mybir
+
+D, POOL, SLOTS, Q = 512, 1024, 512, 128
+FLOPS = 3 * 2 * D * POOL * Q
+
+F32 = mybir.dt.float32
+BF16 = mybir.dt.bfloat16
+I32 = mybir.dt.int32
+U32 = mybir.dt.uint32
+U16 = mybir.dt.uint16
+U8 = mybir.dt.uint8
+FP8X4 = mybir.dt.float8_e4m3fn_x4
+FP4X4 = mybir.dt.float4_e2m1fn_x4
+ALU = mybir.AluOpType
+COPY = mybir.ActivationFunctionType.Copy
+
+P = 128
+PACK = 4
+BANK = 512
+HALF = SLOTS // 2
+LIST_COLS = SLOTS // 16
+HALF_COLS = LIST_COLS // 2
+
+
+def tile_attend_correctedthen_three_kernel(
+    tc, query, keys_words, keys_scales, notes_words, notes_scales, users_words, users_scales,
+    offs, offs2, offs3, offs4, offs5, out,
+):
+    nc = tc.nc
+    with ExitStack() as ctx:
+        lists = ctx.enter_context(tc.tile_pool(name="lists", bufs=1))
+        keep = ctx.enter_context(tc.tile_pool(name="keep", bufs=1))
+        psum = ctx.enter_context(tc.psum_pool(name="psum", bufs=1))
+
+        def zeroed_plane(name):
+            plane = keep.tile([P, POOL], U8, name=name, align_bytes=64)
+            nc.vector.memset(plane[:].bitcast(I32), 0)
+            return plane
+
+        def load_scales(plane, scales):
+            for quad in range(4):
+                nc.sync.dma_start(
+                    plane[32 * quad : 32 * quad + 4, :].bitcast(I32),
+                    scales[0, 4 * quad : 4 * quad + 4, :].bitcast(I32),
+                )
+
+        def load_words(name, words):
+            tile = keep.tile([P, words.shape[1]], U8, name=name, align_bytes=64)
+            nc.sync.dma_start(tile[:].bitcast(I32), words.bitcast(I32))
+            return tile
+
+        def load_list(name, source):
+            tile = lists.tile([P, LIST_COLS], U16, name=name)
+            nc.sync.dma_start(tile[:], source)
+            return tile
+
+        keys_plane = zeroed_plane("keys_plane")
+        notes_plane = zeroed_plane("notes_plane")
+        users_plane = zeroed_plane("users_plane")
+        f1 = keep.tile([P, POOL], F32, name="f1")
+        f2 = keep.tile([P, POOL], F32, name="f2")
+        nc.vector.memset(f1[:], 0.0)
+        nc.vector.memset(f2[:], 0.0)
+
+        raw = keep.tile([P, PACK, Q], F32, name="raw")
+        nc.sync.dma_start(raw[:], query.rearrange("(p j) q -> p j q", j=PACK))
+        keys = load_words("keys", keys_words[0])
+        load_scales(keys_plane, keys_scales)
+        notes = load_words("notes", notes_words[0].rearrange("p n t -> p (n t)"))
+        load_scales(notes_plane, notes_scales)
+        idx = load_list("idx", offs)
+        idx2 = load_list("idx2", offs2)
+        users = load_words("users", users_words[0])
+        load_scales(users_plane, users_scales)
+        idx3 = load_list("idx3", offs3)
+        idx4 = load_list("idx4", offs4)
+        idx5 = load_list("idx5", offs5)
+
+        grouped = keep.tile([P, Q, PACK], BF16, name="grouped", align_bytes=64)
+        nc.vector.tensor_copy(grouped[:], raw[:].rearrange("p j q -> p q j"))
+        q_codes = keep.tile([P, Q], U32, name="q_codes", align_bytes=64)
+        q_plane = keep.tile([P, Q], U8, name="q_plane", align_bytes=64)
+        nc.vector.quantize_mx(
+            out=q_codes[:].bitcast(FP8X4), scales=q_plane[:], in_=grouped[:].rearrange("p q j -> p (q j)")
+        )
+
+        def scores(name, words, plane, dtype):
+            width = words.shape[1] // POOL
+            banks = []
+            for n0 in range(0, POOL, BANK):
+                bank = psum.tile([P, BANK], F32, name="%s_%d" % (name, n0))
+                nc.tensor.matmul_mx(
+                    out=bank[:],
+                    lhsT=q_codes[:].bitcast(FP8X4),
+                    lhsT_scale=q_plane[:],
+                    rhs=words[:, width * n0 : width * (n0 + BANK)].bitcast(dtype),
+                    rhs_scale=plane[:, n0 : n0 + BANK],
+                    start=True,
+                    stop=True,
+                )
+                banks.append(bank)
+            return banks
+
+        a_banks = scores("a_bank", keys, keys_plane, FP4X4)
+        b_banks = scores("b_bank", notes, notes_plane, FP8X4)
+        c_banks = scores("c_bank", users, users_plane, FP4X4)
+
+        a = keep.tile([P, POOL], F32, name="a")
+        b = keep.tile([P, POOL], F32, name="b")
+        nc.vector.tensor_copy(a[:, :BANK], a_banks[0][:])
+        nc.scalar.activation(a[:, BANK:], a_banks[1][:], COPY)
+        nc.vector.tensor_copy(b[:, :BANK], b_banks[0][:])
+        nc.scalar.activation(b[:, BANK:], b_banks[1][:], COPY)
+
+        halves = [slice(0, HALF_COLS), slice(HALF_COLS, LIST_COLS)]
+        minus_a = [keep.tile([P, HALF], F32, name="minus_a%d" % h) for h in range(2)]
+        picked_b = [keep.tile([P, HALF], F32, name="picked_b%d" % h) for h in range(2)]
+        nc.vector.tensor_scalar(minus_a[0][:], a[:].indirect(idx[:, halves[0]]), -1.0, 0.0, ALU.mult, ALU.add)
+        nc.scalar.activation(picked_b[0][:], b[:].indirect(idx2[:, halves[0]]), COPY)
+        nc.scalar.activation(picked_b[1][:], b[:].indirect(idx2[:, halves[1]]), COPY)
+        nc.scalar.activation(minus_a[1][:], a[:].indirect(idx[:, halves[1]]), COPY, scale=-1.0)
+        for h in range(2):
+            nc.vector.tensor_tensor(f1[:].indirect(idx[:, halves[h]]), picked_b[h][:], minus_a[h][:], ALU.add)
+
+        a2 = keep.tile([P, POOL], F32, name="a2")
+        for k in range(2):
+            cols = slice(k * BANK, (k + 1) * BANK)
+            nc.vector.tensor_tensor(a2[:, cols], a_banks[k][:], f1[:, cols], ALU.add)
+
+        picked_a2 = [keep.tile([P, HALF], F32, name="picked_a2%d" % h) for h in range(2)]
+        nc.vector.tensor_copy(picked_a2[0][:], a2[:].indirect(idx3[:, halves[0]]))
+        nc.scalar.activation(picked_a2[1][:], a2[:].indirect(idx3[:, halves[1]]), COPY)
+        for h in range(2):
+            nc.vector.tensor_copy(f2[:].indirect(idx4[:, halves[h]]), picked_a2[h][:])
+
+        cc = keep.tile([P, POOL], F32, name="cc")
+        for k in range(2):
+            cols = slice(k * BANK, (k + 1) * BANK)
+            nc.vector.tensor_tensor(cc[:, cols], c_banks[k][:], f2[:, cols], ALU.subtract)
+
+        result = [keep.tile([P, HALF], F32, name="result%d" % h) for h in range(2)]
+        nc.vector.tensor_copy(result[0][:], cc[:].indirect(idx5[:, halves[0]]))
+        nc.scalar.activation(result[1][:], cc[:].indirect(idx5[:, halves[1]]), COPY)
+        nc.sync.dma_start(out[:, :HALF], result[0][:])
+        nc.scalar.dma_start(out[:, HALF:], result[1][:])

@@ -39,8 +39,8 @@ def tile_attend_correctedthen_three_kernel(
             nc.vector.memset(plane[:].bitcast(I32), 0)
             return plane
 
-        def load_scales(plane, scales):
-            for quad in range(4):
+        def load_scales(plane, scales, quads=range(4)):
+            for quad in quads:
                 nc.sync.dma_start(
                     plane[32 * quad : 32 * quad + 4, :].bitcast(I32),
                     scales[0, 4 * quad : 4 * quad + 4, :].bitcast(I32),
@@ -60,17 +60,16 @@ def tile_attend_correctedthen_three_kernel(
         notes_plane = zeroed_plane("notes_plane")
         users_plane = zeroed_plane("users_plane")
         f1 = keep.tile([P, POOL], F32, name="f1")
-        f2 = keep.tile([P, POOL], F32, name="f2")
         nc.vector.memset(f1[:], 0.0)
-        nc.vector.memset(f2[:], 0.0)
 
         raw = keep.tile([P, PACK, Q], F32, name="raw")
         nc.sync.dma_start(raw[:], query.rearrange("(p j) q -> p j q", j=PACK))
+        idx = load_list("idx", offs)
+        load_scales(keys_plane, keys_scales, range(2))
         keys = load_words("keys", keys_words[0])
-        load_scales(keys_plane, keys_scales)
+        load_scales(keys_plane, keys_scales, range(2, 4))
         notes = load_words("notes", notes_words[0].rearrange("p n t -> p (n t)"))
         load_scales(notes_plane, notes_scales)
-        idx = load_list("idx", offs)
         idx2 = load_list("idx2", offs2)
         users = load_words("users", users_words[0])
         load_scales(users_plane, users_scales)
@@ -78,7 +77,7 @@ def tile_attend_correctedthen_three_kernel(
         idx4 = load_list("idx4", offs4)
         idx5 = load_list("idx5", offs5)
 
-        grouped = keep.tile([P, Q, PACK], BF16, name="grouped", align_bytes=64)
+        grouped = keep.tile([P, Q, PACK], BF16, name="grouped", tag="shared", align_bytes=64)
         nc.vector.tensor_copy(grouped[:], raw[:].rearrange("p j q -> p q j"))
         q_codes = keep.tile([P, Q], U32, name="q_codes", align_bytes=64)
         q_plane = keep.tile([P, Q], U8, name="q_plane", align_bytes=64)
@@ -86,58 +85,60 @@ def tile_attend_correctedthen_three_kernel(
             out=q_codes[:].bitcast(FP8X4), scales=q_plane[:], in_=grouped[:].rearrange("p q j -> p (q j)")
         )
 
-        def scores(name, words, plane, dtype):
-            width = words.shape[1] // POOL
-            banks = []
-            for n0 in range(0, POOL, BANK):
-                bank = psum.tile([P, BANK], F32, name="%s_%d" % (name, n0))
-                nc.tensor.matmul_mx(
-                    out=bank[:],
-                    lhsT=q_codes[:].bitcast(FP8X4),
-                    lhsT_scale=q_plane[:],
-                    rhs=words[:, width * n0 : width * (n0 + BANK)].bitcast(dtype),
-                    rhs_scale=plane[:, n0 : n0 + BANK],
-                    start=True,
-                    stop=True,
-                )
-                banks.append(bank)
-            return banks
+        f2 = keep.tile([P, POOL], F32, name="f2", tag="shared", align_bytes=64)
+        nc.gpsimd.memset(f2[:], 0.0)
 
-        a_banks = scores("a_bank", keys, keys_plane, FP4X4)
-        b_banks = scores("b_bank", notes, notes_plane, FP8X4)
-        c_banks = scores("c_bank", users, users_plane, FP4X4)
+        def scores(words, plane, dtype, cols, tag):
+            width = words.shape[1] // POOL
+            bank = psum.tile([P, cols.stop - cols.start], F32, name="bank", tag=tag)
+            nc.tensor.matmul_mx(
+                out=bank[:],
+                lhsT=q_codes[:].bitcast(FP8X4),
+                lhsT_scale=q_plane[:],
+                rhs=words[:, width * cols.start : width * cols.stop].bitcast(dtype),
+                rhs_scale=plane[:, cols],
+                start=True,
+                stop=True,
+            )
+            return bank
+
+        def to_sbuf(on_vector, dest, bank):
+            if on_vector:
+                nc.vector.tensor_copy(dest, bank[:])
+            else:
+                nc.scalar.activation(dest, bank[:], COPY)
 
         a = keep.tile([P, POOL], F32, name="a")
         b = keep.tile([P, POOL], F32, name="b")
-        nc.vector.tensor_copy(a[:, :BANK], a_banks[0][:])
-        nc.scalar.activation(a[:, BANK:], a_banks[1][:], COPY)
-        nc.vector.tensor_copy(b[:, :BANK], b_banks[0][:])
-        nc.scalar.activation(b[:, BANK:], b_banks[1][:], COPY)
+        a_cols = [slice(n0, n0 + 256) for n0 in range(0, POOL, 256)]
+        a_banks = [scores(keys, keys_plane, FP4X4, cols, "a%d" % k) for k, cols in enumerate(a_cols)]
+        for k, cols in enumerate(a_cols):
+            to_sbuf(k % 2 == 0, a[:, cols], a_banks[k])
+        b_cols = [slice(n0, n0 + 256) for n0 in range(0, POOL, 256)]
+        for k, cols in enumerate(b_cols):
+            to_sbuf(k % 2 == 0, b[:, cols], scores(notes, notes_plane, FP8X4, cols, "b%d" % k))
+        c_cols = [slice(0, 512), slice(512, 1024)]
+        c_banks = [scores(users, users_plane, FP4X4, cols, "b%d" % k) for k, cols in enumerate(c_cols)]
 
         halves = [slice(0, HALF_COLS), slice(HALF_COLS, LIST_COLS)]
-        minus_a = [keep.tile([P, HALF], F32, name="minus_a%d" % h) for h in range(2)]
-        picked_b = [keep.tile([P, HALF], F32, name="picked_b%d" % h) for h in range(2)]
-        nc.vector.tensor_scalar(minus_a[0][:], a[:].indirect(idx[:, halves[0]]), -1.0, 0.0, ALU.mult, ALU.add)
-        nc.scalar.activation(picked_b[0][:], b[:].indirect(idx2[:, halves[0]]), COPY)
-        nc.scalar.activation(picked_b[1][:], b[:].indirect(idx2[:, halves[1]]), COPY)
-        nc.scalar.activation(minus_a[1][:], a[:].indirect(idx[:, halves[1]]), COPY, scale=-1.0)
-        for h in range(2):
-            nc.vector.tensor_tensor(f1[:].indirect(idx[:, halves[h]]), picked_b[h][:], minus_a[h][:], ALU.add)
+        minus_a = keep.tile([P, SLOTS], F32, name="minus_a")
+        picked_b = keep.tile([P, SLOTS], F32, name="picked_b")
+        nc.vector.tensor_scalar(minus_a[:, :HALF], a[:].indirect(idx[:, halves[0]]), -1.0, 0.0, ALU.mult, ALU.add)
+        nc.scalar.activation(minus_a[:, HALF:], a[:].indirect(idx[:, halves[1]]), COPY, scale=-1.0)
+        nc.vector.tensor_copy(picked_b[:, :HALF], b[:].indirect(idx2[:, halves[0]]))
+        nc.scalar.activation(picked_b[:, HALF:], b[:].indirect(idx2[:, halves[1]]), COPY)
+        nc.vector.tensor_tensor(f1[:].indirect(idx[:]), picked_b[:], minus_a[:], ALU.add)
 
         a2 = keep.tile([P, POOL], F32, name="a2")
-        for k in range(2):
-            cols = slice(k * BANK, (k + 1) * BANK)
-            nc.vector.tensor_tensor(a2[:, cols], a_banks[k][:], f1[:, cols], ALU.add)
+        nc.vector.tensor_tensor(a2[:], a[:], f1[:], ALU.add)
 
-        picked_a2 = [keep.tile([P, HALF], F32, name="picked_a2%d" % h) for h in range(2)]
-        nc.vector.tensor_copy(picked_a2[0][:], a2[:].indirect(idx3[:, halves[0]]))
-        nc.scalar.activation(picked_a2[1][:], a2[:].indirect(idx3[:, halves[1]]), COPY)
-        for h in range(2):
-            nc.vector.tensor_copy(f2[:].indirect(idx4[:, halves[h]]), picked_a2[h][:])
+        picked_a2 = keep.tile([P, SLOTS], F32, name="picked_a2")
+        nc.vector.tensor_copy(picked_a2[:, :HALF], a2[:].indirect(idx3[:, halves[0]]))
+        nc.scalar.activation(picked_a2[:, HALF:], a2[:].indirect(idx3[:, halves[1]]), COPY)
+        nc.vector.tensor_copy(f2[:].indirect(idx4[:]), picked_a2[:])
 
         cc = keep.tile([P, POOL], F32, name="cc")
-        for k in range(2):
-            cols = slice(k * BANK, (k + 1) * BANK)
+        for k, cols in enumerate(c_cols):
             nc.vector.tensor_tensor(cc[:, cols], c_banks[k][:], f2[:, cols], ALU.subtract)
 
         result = [keep.tile([P, HALF], F32, name="result%d" % h) for h in range(2)]

@@ -117,7 +117,7 @@ def tile_attend_correctedthen_three_kernel(
         b_cols = [slice(n0, n0 + 256) for n0 in range(0, POOL, 256)]
         for k, cols in enumerate(b_cols):
             to_sbuf(k % 2 == 0, b[:, cols], scores(notes, notes_plane, FP8X4, cols, "b%d" % k))
-        c_cols = [slice(0, 512), slice(512, 1024)]
+        c_cols = [slice(0, 512), slice(512, 768), slice(768, 1024)]
         c_banks = [scores(users, users_plane, FP4X4, cols, "b%d" % k) for k, cols in enumerate(c_cols)]
 
         halves = [slice(0, HALF_COLS), slice(HALF_COLS, LIST_COLS)]
@@ -130,15 +130,20 @@ def tile_attend_correctedthen_three_kernel(
         nc.vector.tensor_tensor(f1[:].indirect(idx[:]), picked_b[:], minus_a[:], ALU.add)
 
         a2 = keep.tile([P, POOL], F32, name="a2")
-        nc.vector.tensor_tensor(a2[:], a[:], f1[:], ALU.add)
+        for k, cols in enumerate(a_cols[:-1]):
+            nc.vector.tensor_tensor(a2[:, cols], a_banks[k][:], f1[:, cols], ALU.add)
+        nc.gpsimd.tensor_tensor(a2[:, a_cols[-1]], a[:, a_cols[-1]], f1[:, a_cols[-1]], ALU.add)
 
         picked_a2 = keep.tile([P, SLOTS], F32, name="picked_a2")
         nc.vector.tensor_copy(picked_a2[:, :HALF], a2[:].indirect(idx3[:, halves[0]]))
         nc.scalar.activation(picked_a2[:, HALF:], a2[:].indirect(idx3[:, halves[1]]), COPY)
         nc.vector.tensor_copy(f2[:].indirect(idx4[:]), picked_a2[:])
 
+        c_last = keep.tile([P, 256], F32, name="c_last")
+        nc.scalar.activation(c_last[:], c_banks[-1][:], COPY)
         cc = keep.tile([P, POOL], F32, name="cc")
-        for k, cols in enumerate(c_cols):
+        nc.gpsimd.tensor_tensor(cc[:, c_cols[-1]], c_last[:], f2[:, c_cols[-1]], ALU.subtract)
+        for k, cols in enumerate(c_cols[:-1]):
             nc.vector.tensor_tensor(cc[:, cols], c_banks[k][:], f2[:, cols], ALU.subtract)
 
         result = [keep.tile([P, HALF], F32, name="result%d" % h) for h in range(2)]

@@ -116,15 +116,14 @@ def tile_attend_correctedthen_three_kernel(
             to_sbuf(k % 2 == 0, a[:, cols], a_banks[k])
         b_cols = [slice(n0, n0 + 256) for n0 in range(0, POOL, 256)]
         for k, cols in enumerate(b_cols):
-            to_sbuf(k % 2 == 0, b[:, cols], scores(notes, notes_plane, FP8X4, cols, "b%d" % k))
+            to_sbuf(True, b[:, cols], scores(notes, notes_plane, FP8X4, cols, "b%d" % k))
         c_cols = [slice(0, 512), slice(512, 768), slice(768, 1024)]
         c_banks = [scores(users, users_plane, FP4X4, cols, "b%d" % k) for k, cols in enumerate(c_cols)]
 
         halves = [slice(0, HALF_COLS), slice(HALF_COLS, LIST_COLS)]
         minus_a = keep.tile([P, SLOTS], F32, name="minus_a")
         picked_b = keep.tile([P, SLOTS], F32, name="picked_b")
-        nc.vector.tensor_scalar(minus_a[:, :HALF], a[:].indirect(idx[:, halves[0]]), -1.0, 0.0, ALU.mult, ALU.add)
-        nc.scalar.activation(minus_a[:, HALF:], a[:].indirect(idx[:, halves[1]]), COPY, scale=-1.0)
+        nc.scalar.activation(minus_a[:], a[:].indirect(idx[:]), COPY, scale=-1.0)
         nc.vector.tensor_copy(picked_b[:, :HALF], b[:].indirect(idx2[:, halves[0]]))
         nc.scalar.activation(picked_b[:, HALF:], b[:].indirect(idx2[:, halves[1]]), COPY)
         nc.vector.tensor_tensor(f1[:].indirect(idx[:]), picked_b[:], minus_a[:], ALU.add)

from contextlib import ExitStack

import concourse.mybir as mybir

D, POOL, SLOTS, Q = 512, 1024, 512, 128
FLOPS = 3 * 2 * D * POOL * Q

F32 = mybir.dt.float32
BF16 = mybir.dt.bfloat16
I32 = mybir.dt.int32
U32 = mybir.dt.uint32
U16 = mybir.dt.uint16
U8 = mybir.dt.uint8
FP8X4 = mybir.dt.float8_e4m3fn_x4
FP4X4 = mybir.dt.float4_e2m1fn_x4
ALU = mybir.AluOpType
COPY = mybir.ActivationFunctionType.Copy

P = 128
PACK = 4
BANK = 512
HALF = SLOTS // 2
LIST_COLS = SLOTS // 16
HALF_COLS = LIST_COLS // 2


def tile_attend_correctedthen_three_kernel(
    tc, query, keys_words, keys_scales, notes_words, notes_scales, users_words, users_scales,
    offs, offs2, offs3, offs4, offs5, out,
):
    nc = tc.nc
    with ExitStack() as ctx:
        lists = ctx.enter_context(tc.tile_pool(name="lists", bufs=1))
        keep = ctx.enter_context(tc.tile_pool(name="keep", bufs=1))
        psum = ctx.enter_context(tc.psum_pool(name="psum", bufs=1))

        def zeroed_plane(name):
            plane = keep.tile([P, POOL], U8, name=name, align_bytes=64)
            nc.vector.memset(plane[:].bitcast(I32), 0)
            return plane

        def load_scales(plane, scales, quads=range(4)):
            for quad in quads:
                nc.sync.dma_start(
                    plane[32 * quad : 32 * quad + 4, :].bitcast(I32),
                    scales[0, 4 * quad : 4 * quad + 4, :].bitcast(I32),
                )

        def load_words(name, words):
            tile = keep.tile([P, words.shape[1]], U8, name=name, align_bytes=64)
            nc.sync.dma_start(tile[:].bitcast(I32), words.bitcast(I32))
            return tile

        def load_list(name, source):
            tile = lists.tile([P, LIST_COLS], U16, name=name)
            nc.sync.dma_start(tile[:], source)
            return tile

        keys_plane = zeroed_plane("keys_plane")
        notes_plane = zeroed_plane("notes_plane")
        users_plane = zeroed_plane("users_plane")
        f1 = keep.tile([P, POOL], F32, name="f1")
        nc.vector.memset(f1[:], 0.0)

        raw = keep.tile([P, PACK, Q], F32, name="raw")
        nc.sync.dma_start(raw[:], query.rearrange("(p j) q -> p j q", j=PACK))
        idx = load_list("idx", offs)
        load_scales(keys_plane, keys_scales, range(2))
        keys = load_words("keys", keys_words[0])
        load_scales(keys_plane, keys_scales, range(2, 4))
        notes = load_words("notes", notes_words[0].rearrange("p n t -> p (n t)"))
        load_scales(notes_plane, notes_scales)
        idx2 = load_list("idx2", offs2)
        users = load_words("users", users_words[0])
        load_scales(users_plane, users_scales)
        idx3 = load_list("idx3", offs3)
        idx4 = load_list("idx4", offs4)
        idx5 = load_list("idx5", offs5)

        grouped = keep.tile([P, Q, PACK], BF16, name="grouped", tag="shared", align_bytes=64)
        nc.vector.tensor_copy(grouped[:], raw[:].rearrange("p j q -> p q j"))
        q_codes = keep.tile([P, Q], U32, name="q_codes", align_bytes=64)
        q_plane = keep.tile([P, Q], U8, name="q_plane", align_bytes=64)
        nc.vector.quantize_mx(
            out=q_codes[:].bitcast(FP8X4), scales=q_plane[:], in_=grouped[:].rearrange("p q j -> p (q j)")
        )

        f2 = keep.tile([P, POOL], F32, name="f2", tag="shared", align_bytes=64)
        nc.gpsimd.memset(f2[:], 0.0)

        def scores(words, plane, dtype, cols, tag):
            width = words.shape[1] // POOL
            bank = psum.tile([P, cols.stop - cols.start], F32, name="bank", tag=tag)
            nc.tensor.matmul_mx(
                out=bank[:],
                lhsT=q_codes[:].bitcast(FP8X4),
                lhsT_scale=q_plane[:],
                rhs=words[:, width * cols.start : width * cols.stop].bitcast(dtype),
                rhs_scale=plane[:, cols],
                start=True,
                stop=True,
            )
            return bank

        def to_sbuf(on_vector, dest, bank):
            if on_vector:
                nc.vector.tensor_copy(dest, bank[:])
            else:
                nc.scalar.activation(dest, bank[:], COPY)

        a = keep.tile([P, POOL], F32, name="a")
        b = keep.tile([P, POOL], F32, name="b")
        a_cols = [slice(n0, n0 + 256) for n0 in range(0, POOL, 256)]
        a_banks = [scores(keys, keys_plane, FP4X4, cols, "a%d" % k) for k, cols in enumerate(a_cols)]
        for k, cols in enumerate(a_cols):
            to_sbuf(k % 2 == 0, a[:, cols], a_banks[k])
        b_cols = [slice(n0, n0 + 256) for n0 in range(0, POOL, 256)]
        for k, cols in enumerate(b_cols):
            to_sbuf(True, b[:, cols], scores(notes, notes_plane, FP8X4, cols, "b%d" % k))
        c_cols = [slice(0, 512), slice(512, 768), slice(768, 1024)]
        c_banks = [scores(users, users_plane, FP4X4, cols, "b%d" % k) for k, cols in enumerate(c_cols)]

        halves = [slice(0, HALF_COLS), slice(HALF_COLS, LIST_COLS)]
        minus_a = keep.tile([P, SLOTS], F32, name="minus_a")
        picked_b = keep.tile([P, SLOTS], F32, name="picked_b")
        nc.scalar.activation(minus_a[:], a[:].indirect(idx[:]), COPY, scale=-1.0)
        nc.vector.tensor_copy(picked_b[:, :HALF], b[:].indirect(idx2[:, halves[0]]))
        nc.scalar.activation(picked_b[:, HALF:], b[:].indirect(idx2[:, halves[1]]), COPY)
        nc.vector.tensor_tensor(f1[:].indirect(idx[:]), picked_b[:], minus_a[:], ALU.add)

        a2 = keep.tile([P, POOL], F32, name="a2")
        for k, cols in enumerate(a_cols[:-1]):
            nc.vector.tensor_tensor(a2[:, cols], a_banks[k][:], f1[:, cols], ALU.add)
        nc.gpsimd.tensor_tensor(a2[:, a_cols[-1]], a[:, a_cols[-1]], f1[:, a_cols[-1]], ALU.add)

        picked_a2 = keep.tile([P, SLOTS], F32, name="picked_a2")
        nc.vector.tensor_copy(picked_a2[:, :HALF], a2[:].indirect(idx3[:, halves[0]]))
        nc.scalar.activation(picked_a2[:, HALF:], a2[:].indirect(idx3[:, halves[1]]), COPY)
        nc.vector.tensor_copy(f2[:].indirect(idx4[:]), picked_a2[:])

        c_last = keep.tile([P, 256], F32, name="c_last")
        nc.scalar.activation(c_last[:], c_banks[-1][:], COPY)
        cc = keep.tile([P, POOL], F32, name="cc")
        nc.gpsimd.tensor_tensor(cc[:, c_cols[-1]], c_last[:], f2[:, c_cols[-1]], ALU.subtract)
        for k, cols in enumerate(c_cols[:-1]):
            nc.vector.tensor_tensor(cc[:, cols], c_banks[k][:], f2[:, cols], ALU.subtract)

        result = [keep.tile([P, HALF], F32, name="result%d" % h) for h in range(2)]
        nc.vector.tensor_copy(result[0][:], cc[:].indirect(idx5[:, halves[0]]))
        nc.scalar.activation(result[1][:], cc[:].indirect(idx5[:, halves[1]]), COPY)
        nc.sync.dma_start(out[:, :HALF], result[0][:])
        nc.scalar.dma_start(out[:, HALF:], result[1][:])
